import numpy as np
import ml_dtypes


def mxq(x, axis, fmt="e4m3"):
    dtype, down = {"e4m3": (ml_dtypes.float8_e4m3fn, 7), "e5m2": (ml_dtypes.float8_e5m2, 14)}[fmt]
    v = np.moveaxis(np.asarray(x, np.float32).astype(ml_dtypes.bfloat16).astype(np.float64), axis, -1)
    blocks = v.reshape(v.shape[:-1] + (-1, 32))
    amax = np.abs(blocks).max(-1, keepdims=True)
    byte = np.maximum(np.where(amax > 0, np.frexp(amax)[1] - 1 + 127, 0) - down, 1)
    scale = np.exp2(byte - 127.0)
    codes = (blocks / scale).astype(np.float32).astype(dtype).astype(np.float64)
    return np.moveaxis((codes * scale).reshape(v.shape), -1, axis)


WIDE = False


def mx_kscale(k, group=512):
    if not WIDE:
        return np.ones(k)
    levels = np.array([10, -10, 5, -5, 0])
    if group != 512:
        return np.exp2(np.random.permutation(np.resize(levels, k // group))).repeat(group)
    if k % 512:
        return np.exp2(np.random.permutation(np.resize(levels, k // 32))).repeat(32)
    a = np.empty((k // 512, 16))
    for p in range(k // 512):
        a[p, :8] = np.random.permutation(np.resize(levels, 8))
        for g in range(8):
            far = levels[np.abs(levels - a[p, g]) >= 10]
            a[p, g + 8] = far[np.random.randint(len(far))]
    return np.exp2(a.ravel()).repeat(32)


def f64(x):
    return np.asarray(x).astype(np.float64)


def striped(idx):
    return np.tile(np.asarray(idx).reshape(-1, 16).T, (8, 1)).astype(np.uint16)


def unstriped(offs):
    return offs[:16].T.reshape(-1).astype(np.int64)


H, KV, D, NQ, N = 4, 4, 256, 512, 512


def setup_inputs():
    n = np.random.standard_normal
    s = mx_kscale(D, 0)[:, None]
    u = mx_kscale(N)
    t = np.random.uniform(0.5, 2.0, N) * u
    v = n((KV, N, 128))
    return {
        "qT": (n((H, D, NQ)) * s * (0.70 / np.sqrt(D))).astype(np.float32),
        "kT": (n((KV, D, N)) / s).astype(np.float32),
        "t": t.reshape(N, 1).astype(np.float32),
        "v": (v / t[:, None]).astype(np.float32),
        "mask": (np.arange(N)[:, None] <= np.sort(np.random.randint(N // 4, N, NQ))[None, :]).astype(np.float32),
        "gn": np.tile(np.random.uniform(0.5, 2.0, 128), (128, 1)).astype(np.float32),
    }


def reference(qT, kT, t, v, mask, gn):
    a = mxq(f64(kT), 1, "e4m3").transpose(0, 2, 1) @ mxq(f64(qT), 1, "e4m3")
    p = 1.0 / (1.0 + np.exp(-a))
    p = p * f64(mask)
    w = p * f64(t)
    y = mxq(w, 1, "e4m3").transpose(0, 2, 1) @ mxq(f64(v), 1, "e4m3")
    y = y / 16.0
    y = y / np.sqrt(np.mean(np.square(y), -1, keepdims=True) + 1e-5) * f64(gn)[:1]
    return y

@@ -1,0 +1,231 @@
+from contextlib import ExitStack
+
+import concourse.mybir as mybir
+
+H, D, NQ, N, E = 4, 256, 512, 512, 128
+FLOPS = 2 * H * N * NQ * (D + E)
+
+F32 = mybir.dt.float32
+BF16 = mybir.dt.bfloat16
+U32 = mybir.dt.uint32
+U8 = mybir.dt.uint8
+FP8X4 = mybir.dt.float8_e4m3fn_x4
+ACT = mybir.ActivationFunctionType
+ALU = mybir.AluOpType
+
+P = 128
+PACK = 4
+ROWS = D // PACK
+QB = 128
+HALF = 256
+EPS = 1e-5
+
+
+def tile_rows_a_sigmoid_mask_onorm_kernel(tc, qT, kT, t, v, mask, gn, out):
+    nc = tc.nc
+    with ExitStack() as ctx:
+        sb = ctx.enter_context(tc.tile_pool(name="sb", bufs=1))
+        ps = ctx.enter_context(tc.psum_pool(name="ps", bufs=1))
+        ctx.enter_context(tc.manual_schedule())
+
+        def sbuf(name, shape, dtype):
+            return sb.tile(shape, dtype, name=name, align_bytes=64)
+
+        def mx_tiles(name, cols):
+            return (sbuf(name + "_bf", [P, PACK * cols], BF16), sbuf(name + "_codes", [P, cols], U32),
+                    sbuf(name + "_scales", [P, cols], U8))
+
+        k_raw = [sbuf("k_raw%d" % g, [P, PACK, N], F32) for g in range(2)]
+        q_raw = [[sbuf("q_raw%d%d" % (g, u), [P, PACK, HALF], F32) for u in range(2)] for g in range(2)]
+        m_raw = [sbuf("m_raw%d" % u, [P, PACK, HALF], F32) for u in range(2)]
+        mt = [sbuf("mt%d" % u, [P, PACK, HALF], F32) for u in range(2)]
+        v_raw = [sbuf("v_raw%d" % g, [P, 2, PACK * E], F32) for g in range(2)]
+        t_sb = sbuf("t_sb", [P, PACK], F32)
+        gn_sb = sbuf("gn_sb", [P, E], F32)
+        k_mx = [[mx_tiles("k%d%d" % (g, a), 2 * P) for a in range(2)] for g in range(2)]
+        q_mx = [[mx_tiles("q%d%d" % (g, b), QB) for b in range(4)] for g in range(2)]
+        v_mx = [mx_tiles("v%d" % g, 2 * E) for g in range(2)]
+        w_mx = [mx_tiles("w%d" % n, QB) for n in range(16)]
+        p_sb = [sbuf("p%d" % n, [P, PACK * QB], F32) for n in range(16)]
+        sq_sb = [sbuf("sq%d" % n, [P, E], F32) for n in range(16)]
+        ssq = [sbuf("ssq%d" % f, [P, 4], F32) for f in range(4)]
+        rstd = [sbuf("rstd%d" % f, [P, 4], F32) for f in range(4)]
+        o_sb = [[sbuf("o%d%d" % (f, a), [P, 2, E], F32) for a in range(2)] for f in range(4)]
+        score = [[ps.tile([P, PACK, QB], F32, name="score%d%d" % (a, b)) for b in range(2)] for a in range(2)]
+        y_ps = [ps.tile([P, 4, E], F32, name="y%d" % f) for f in range(4)]
+
+        def load_pair(src, g, cols, dst):
+            rows = src[2 * g:2 * g + 2].rearrange("h (p j) c -> (h p) j c", j=PACK)
+            nc.sync.dma_start(out=dst[:], in_=rows[:, :, cols])
+
+        def load_q(g, u):
+            load_pair(qT, g, slice(HALF * u, HALF * (u + 1)), q_raw[g][u])
+
+        def load_mask(u):
+            nc.sync.dma_start(out=m_raw[u][:],
+                              in_=mask.rearrange("(p r) q -> p r q", r=PACK)[:, :, HALF * u:HALF * (u + 1)])
+
+        def load_v(g):
+            nc.sync.dma_start(out=v_raw[g][:],
+                              in_=v[2 * g:2 * g + 2].rearrange("h (p r) e -> p h (r e)", r=PACK))
+
+        def copy(on_scalar, dst, src):
+            if on_scalar:
+                nc.scalar.copy(out=dst, in_=src)
+            else:
+                nc.vector.tensor_copy(out=dst, in_=src)
+
+        def pack_k(g, a, on_scalar):
+            src = k_raw[g][:].rearrange("p j (s a r) -> p a s j r", a=2, r=2)[:, a]
+            dst = k_mx[g][a][0][:].rearrange("p (r s j) -> p s j r", r=2, j=PACK)
+            copy(on_scalar, dst, src)
+
+        def pack_q(g, b, on_scalar):
+            src = q_raw[g][b // 2][:, :, QB * (b % 2):QB * (b % 2 + 1)].rearrange("p j (c i) -> p c j i", i=2)
+            dst = q_mx[g][b][0][:].rearrange("p (c i j) -> p c j i", i=2, j=PACK)
+            copy(on_scalar, dst, src)
+
+        def pack_v(g, a, on_scalar):
+            src = v_raw[g][:, a, :].rearrange("p (r c i) -> p c r i", r=PACK, i=2)
+            dst = v_mx[g][0][:, PACK * E * a:PACK * E * (a + 1)].rearrange("p (c i r) -> p c r i", i=2, r=PACK)
+            copy(on_scalar, dst, src)
+
+        def quantize(tiles):
+            nc.vector.quantize_mx(out=tiles[1][:].bitcast(FP8X4), scales=tiles[2][:], in_=tiles[0][:])
+
+        def mask_times_t(u):
+            for r in range(PACK):
+                nc.vector.tensor_scalar(out=mt[u][:, r, :], in0=m_raw[u][:, r, :], scalar1=t_sb[:, r:r + 1],
+                                        scalar2=None, op0=ALU.mult)
+
+        def place(n):
+            return n // 8, (n // 2) % 4, n % 2
+
+        def scores(n):
+            g, b, a = place(n)
+            rows = slice(ROWS * a, ROWS * (a + 1))
+            for r in range(PACK):
+                kk = k_mx[g][r // 2]
+                cols = slice(P * (r % 2), P * (r % 2 + 1))
+                nc.tensor.matmul_mx(out=score[a][b % 2][:, r, :],
+                                    lhsT=kk[1][rows, cols].bitcast(FP8X4), lhsT_scale=kk[2][rows, cols],
+                                    rhs=q_mx[g][b][1][rows, :].bitcast(FP8X4), rhs_scale=q_mx[g][b][2][rows, :],
+                                    start=True, stop=True)
+
+        def sigmoid(n):
+            g, b, a = place(n)
+            nc.scalar.activation(out=p_sb[n][:].rearrange("p (c r i) -> p c r i", r=PACK, i=2),
+                                 in_=score[a][b % 2][:].rearrange("p r (c i) -> p c r i", i=2), func=ACT.Sigmoid)
+
+        def weigh(n):
+            g, b, a = place(n)
+            nc.vector.tensor_tensor(
+                out=w_mx[n][0][:].rearrange("p (c i r) -> p c r i", i=2, r=PACK),
+                in0=p_sb[n][:].rearrange("p (c r i) -> p c r i", r=PACK, i=2),
+                in1=mt[b // 2][:, :, QB * (b % 2):QB * (b % 2 + 1)].rearrange("p r (c i) -> p c r i", i=2),
+                op=ALU.mult)
+
+        def values(n):
+            g, b, a = place(n)
+            cols = slice(E * a, E * (a + 1))
+            nc.tensor.matmul_mx(out=y_ps[n // 4][:, n % 4, :],
+                                lhsT=w_mx[n][1][:].bitcast(FP8X4), lhsT_scale=w_mx[n][2][:],
+                                rhs=v_mx[g][1][:, cols].bitcast(FP8X4), rhs_scale=v_mx[g][2][:, cols],
+                                start=True, stop=True)
+
+        def squares(f):
+            for n in range(4 * f, 4 * f + 4):
+                nc.scalar.activation(out=sq_sb[n][:], in_=y_ps[f][:, n % 4, :], func=ACT.Square,
+                                     accum_out=ssq[f][:, n % 4:n % 4 + 1])
+
+        def inverse_root(f):
+            nc.scalar.activation(out=rstd[f][:], in_=ssq[f][:], func=ACT.Abs_reciprocal_sqrt,
+                                 scale=1.0 / E, bias=256.0 * EPS)
+
+        def finish(f):
+            for a in range(2):
+                for b in range(2):
+                    m = 2 * b + a
+                    nc.vector.scalar_tensor_tensor(out=o_sb[f][a][:, b, :], in0=y_ps[f][:, m, :],
+                                                   scalar=rstd[f][:, m:m + 1], in1=gn_sb[:],
+                                                   op0=ALU.mult, op1=ALU.mult)
+                rows = out[2 * (f // 2) + a, HALF * (f % 2):HALF * (f % 2 + 1), :]
+                nc.sync.dma_start(out=rows.rearrange("(b p) e -> p b e", b=2), in_=o_sb[f][a][:])
+
+        nc.scalar.dma_start(out=t_sb[:], in_=t.rearrange("(p r) o -> p (r o)", r=PACK))
+        load_pair(kT, 0, slice(0, N), k_raw[0])
+        load_q(0, 0)
+        load_mask(0)
+        load_q(0, 1)
+        load_mask(1)
+        load_pair(kT, 1, slice(0, N), k_raw[1])
+        load_q(1, 0)
+        load_q(1, 1)
+        load_v(0)
+        load_v(1)
+        nc.sync.dma_start(out=gn_sb[:], in_=gn[:, :])
+
+        pack_k(0, 0, False)
+        pack_k(0, 1, True)
+        quantize(k_mx[0][0])
+        quantize(k_mx[0][1])
+        pack_q(0, 0, False)
+        pack_q(0, 1, True)
+        quantize(q_mx[0][0])
+        scores(0)
+        scores(1)
+        quantize(q_mx[0][1])
+        scores(2)
+        scores(3)
+        mask_times_t(0)
+
+        scalar_side = {
+            2: [lambda: pack_q(0, 2, True)],
+            3: [lambda: pack_q(0, 3, True)],
+            6: [lambda: pack_k(1, 1, True)],
+            7: [lambda: pack_q(1, 1, True)],
+            9: [lambda: pack_q(1, 2, True)],
+            10: [lambda: pack_q(1, 3, True)],
+        }
+        vector_side = {
+            2: [lambda: quantize(q_mx[0][2])],
+            3: [lambda: quantize(q_mx[0][3]), lambda: mask_times_t(1)],
+            5: [lambda: pack_k(1, 0, False)],
+            6: [lambda: quantize(k_mx[1][0]), lambda: pack_q(1, 0, False), lambda: quantize(k_mx[1][1]),
+                lambda: quantize(q_mx[1][0])],
+            7: [lambda: quantize(q_mx[1][1])],
+            9: [lambda: quantize(q_mx[1][2])],
+            10: [lambda: quantize(q_mx[1][3]), lambda: pack_v(0, 0, False), lambda: pack_v(0, 1, False)],
+            11: [lambda: quantize(v_mx[0]), lambda: pack_v(1, 0, False), lambda: pack_v(1, 1, False)],
+            12: [lambda: quantize(v_mx[1])],
+        }
+        for n in range(16):
+            for job in scalar_side.get(n, []):
+                job()
+            sigmoid(n)
+            for job in vector_side.get(n, []):
+                job()
+            if 4 <= n + 2 < 16:
+                scores(n + 2)
+            weigh(n)
+            if n >= 1:
+                quantize(w_mx[n - 1])
+            if n == 13:
+                for m in range(12):
+                    values(m)
+                squares(0)
+            if n == 14:
+                squares(1)
+        quantize(w_mx[15])
+        for m in range(12, 16):
+            values(m)
+        inverse_root(0)
+        inverse_root(1)
+        finish(0)
+        squares(2)
+        inverse_root(2)
+        finish(1)
+        squares(3)
+        inverse_root(3)
+        finish(2)
+        finish(3)

@@ -17,7 +17,11 @@ P = 128
 PACK = 4
 ROWS = D // PACK
 QB = 128
-HALF = 256
+HALF = 2 * QB
+PAIRS = H // 2
+PHASES = 4
+UNITS = 16
+Y_DIVISOR = 16.0
 EPS = 1e-5
 
 
@@ -35,197 +39,223 @@ def tile_rows_a_sigmoid_mask_onorm_kernel(tc, qT, kT, t, v, mask, gn, out):
             return (sbuf(name + "_bf", [P, PACK * cols], BF16), sbuf(name + "_codes", [P, cols], U32),
                     sbuf(name + "_scales", [P, cols], U8))
 
-        k_raw = [sbuf("k_raw%d" % g, [P, PACK, N], F32) for g in range(2)]
-        q_raw = [[sbuf("q_raw%d%d" % (g, u), [P, PACK, HALF], F32) for u in range(2)] for g in range(2)]
-        m_raw = [sbuf("m_raw%d" % u, [P, PACK, HALF], F32) for u in range(2)]
+        k_raw = [sbuf("k_raw%d" % g, [P, PACK, N], F32) for g in range(PAIRS)]
+        q_raw = [sbuf("q_raw%d" % g, [P, PACK, NQ], F32) for g in range(PAIRS)]
+        v_raw = [sbuf("v_raw%d" % g, [P, 2, PACK * E], F32) for g in range(PAIRS)]
+        m_raw = [sbuf("m_raw%d" % rh, [P, 2, NQ], F32) for rh in range(2)]
         mt = [sbuf("mt%d" % u, [P, PACK, HALF], F32) for u in range(2)]
-        v_raw = [sbuf("v_raw%d" % g, [P, 2, PACK * E], F32) for g in range(2)]
         t_sb = sbuf("t_sb", [P, PACK], F32)
         gn_sb = sbuf("gn_sb", [P, E], F32)
-        k_mx = [[mx_tiles("k%d%d" % (g, a), 2 * P) for a in range(2)] for g in range(2)]
-        q_mx = [[mx_tiles("q%d%d" % (g, b), QB) for b in range(4)] for g in range(2)]
-        v_mx = [mx_tiles("v%d" % g, 2 * E) for g in range(2)]
-        w_mx = [mx_tiles("w%d" % n, QB) for n in range(16)]
-        p_sb = [sbuf("p%d" % n, [P, PACK * QB], F32) for n in range(16)]
-        sq_sb = [sbuf("sq%d" % n, [P, E], F32) for n in range(16)]
-        ssq = [sbuf("ssq%d" % f, [P, 4], F32) for f in range(4)]
-        rstd = [sbuf("rstd%d" % f, [P, 4], F32) for f in range(4)]
-        o_sb = [[sbuf("o%d%d" % (f, a), [P, 2, E], F32) for a in range(2)] for f in range(4)]
-        score = [[ps.tile([P, PACK, QB], F32, name="score%d%d" % (a, b)) for b in range(2)] for a in range(2)]
-        y_ps = [ps.tile([P, 4, E], F32, name="y%d" % f) for f in range(4)]
+        k_mx = [[mx_tiles("k%d%d" % (g, rh), 2 * P) for rh in range(2)] for g in range(PAIRS)]
+        q_mx = [[mx_tiles("q%d%d" % (g, b), QB) for b in range(NQ // QB)] for g in range(PAIRS)]
+        v_mx = [mx_tiles("v%d" % g, 2 * E) for g in range(PAIRS)]
+        w_mx = [[mx_tiles("w%d%d" % (f, a), HALF) for a in range(2)] for f in range(PHASES)]
+        p_sb = [sbuf("p%d" % n, [P, PACK * QB], F32) for n in range(UNITS)]
+        y_squared = [sbuf("y_squared%d" % n, [P, E], F32) for n in range(UNITS)]
+        sum_squares = [sbuf("sum_squares%d" % f, [P, 4], F32) for f in range(PHASES)]
+        inv_root = [sbuf("inv_root%d" % f, [P, 4], F32) for f in range(PHASES)]
+        o_sb = [[sbuf("o%d%d" % (f, a), [P, 2 * E], F32) for a in range(2)] for f in range(PHASES)]
+        warm_in = sbuf("warm_in", [P, 8], F32)
+        warm_out = sbuf("warm_out", [P, 8], F32)
+        score = [[ps.tile([P, PACK, QB], F32, name="score%d%d" % (a, x)) for x in range(2)] for a in range(2)]
+        y_ps = [ps.tile([P, 4, E], F32, name="y%d" % f) for f in range(PHASES)]
 
-        def load_pair(src, g, cols, dst):
+        def load_features(src, g, dst):
             rows = src[2 * g:2 * g + 2].rearrange("h (p j) c -> (h p) j c", j=PACK)
-            nc.sync.dma_start(out=dst[:], in_=rows[:, :, cols])
+            nc.sync.dma_start(out=dst[:], in_=rows)
 
-        def load_q(g, u):
-            load_pair(qT, g, slice(HALF * u, HALF * (u + 1)), q_raw[g][u])
-
-        def load_mask(u):
-            nc.sync.dma_start(out=m_raw[u][:],
-                              in_=mask.rearrange("(p r) q -> p r q", r=PACK)[:, :, HALF * u:HALF * (u + 1)])
+        def load_mask(rh):
+            rows = mask.rearrange("(s r) q -> s r q", r=PACK)[:, 2 * rh:2 * rh + 2, :]
+            nc.sync.dma_start(out=m_raw[rh][:], in_=rows)
 
         def load_v(g):
-            nc.sync.dma_start(out=v_raw[g][:],
-                              in_=v[2 * g:2 * g + 2].rearrange("h (p r) e -> p h (r e)", r=PACK))
+            nc.sync.dma_start(out=v_raw[g][:], in_=v[2 * g:2 * g + 2].rearrange("h (s r) e -> s h (r e)", r=PACK))
 
-        def copy(on_scalar, dst, src):
-            if on_scalar:
-                nc.scalar.copy(out=dst, in_=src)
-            else:
-                nc.vector.tensor_copy(out=dst, in_=src)
+        def on_vector(dst, src):
+            nc.vector.tensor_copy(out=dst, in_=src)
 
-        def pack_k(g, a, on_scalar):
-            src = k_raw[g][:].rearrange("p j (s a r) -> p a s j r", a=2, r=2)[:, a]
-            dst = k_mx[g][a][0][:].rearrange("p (r s j) -> p s j r", r=2, j=PACK)
-            copy(on_scalar, dst, src)
+        def on_scalar(dst, src):
+            nc.scalar.copy(out=dst, in_=src)
 
-        def pack_q(g, b, on_scalar):
-            src = q_raw[g][b // 2][:, :, QB * (b % 2):QB * (b % 2 + 1)].rearrange("p j (c i) -> p c j i", i=2)
-            dst = q_mx[g][b][0][:].rearrange("p (c i j) -> p c j i", i=2, j=PACK)
-            copy(on_scalar, dst, src)
+        def pack_k(g, rh, copy):
+            src = k_raw[g][:].rearrange("p j (s rh x) -> p rh s j x", rh=2, x=2)[:, rh]
+            copy(k_mx[g][rh][0][:].rearrange("p (x s j) -> p s j x", x=2, j=PACK), src)
 
-        def pack_v(g, a, on_scalar):
-            src = v_raw[g][:, a, :].rearrange("p (r c i) -> p c r i", r=PACK, i=2)
-            dst = v_mx[g][0][:, PACK * E * a:PACK * E * (a + 1)].rearrange("p (c i r) -> p c r i", i=2, r=PACK)
-            copy(on_scalar, dst, src)
+        def pack_q(g, b, copy):
+            src = q_raw[g][:, :, QB * b:QB * (b + 1)].rearrange("p j (c x) -> p c j x", x=2)
+            copy(q_mx[g][b][0][:].rearrange("p (c x j) -> p c j x", x=2, j=PACK), src)
 
-        def quantize(tiles):
-            nc.vector.quantize_mx(out=tiles[1][:].bitcast(FP8X4), scales=tiles[2][:], in_=tiles[0][:])
+        def pack_v(g, a, copy):
+            src = v_raw[g][:, a, :].rearrange("s (r c x) -> s c r x", r=PACK, x=2)
+            dst = v_mx[g][0][:, PACK * E * a:PACK * E * (a + 1)]
+            copy(dst.rearrange("s (c x r) -> s c r x", x=2, r=PACK), src)
 
-        def mask_times_t(u):
-            for r in range(PACK):
-                nc.vector.tensor_scalar(out=mt[u][:, r, :], in0=m_raw[u][:, r, :], scalar1=t_sb[:, r:r + 1],
-                                        scalar2=None, op0=ALU.mult)
+        def quantize(operand):
+            values_bf, codes, scales = operand
+            nc.vector.quantize_mx(out=codes[:].bitcast(FP8X4), scales=scales[:], in_=values_bf[:])
+
+        def mask_times_t(rh, u):
+            for x in range(2):
+                r = 2 * rh + x
+                nc.vector.tensor_scalar(out=mt[u][:, r, :], in0=m_raw[rh][:, x, HALF * u:HALF * (u + 1)],
+                                        scalar1=t_sb[:, r:r + 1], scalar2=None, op0=ALU.mult)
 
         def place(n):
             return n // 8, (n // 2) % 4, n % 2
 
-        def scores(n):
+        def sigmoid_scores(n):
             g, b, a = place(n)
+            bank = score[a][b % 2]
             rows = slice(ROWS * a, ROWS * (a + 1))
+            q_codes, q_scales = q_mx[g][b][1], q_mx[g][b][2]
             for r in range(PACK):
-                kk = k_mx[g][r // 2]
+                k_codes, k_scales = k_mx[g][r // 2][1], k_mx[g][r // 2][2]
                 cols = slice(P * (r % 2), P * (r % 2 + 1))
-                nc.tensor.matmul_mx(out=score[a][b % 2][:, r, :],
-                                    lhsT=kk[1][rows, cols].bitcast(FP8X4), lhsT_scale=kk[2][rows, cols],
-                                    rhs=q_mx[g][b][1][rows, :].bitcast(FP8X4), rhs_scale=q_mx[g][b][2][rows, :],
+                nc.tensor.matmul_mx(out=bank[:, r, :],
+                                    lhsT=k_codes[rows, cols].bitcast(FP8X4), lhsT_scale=k_scales[rows, cols],
+                                    rhs=q_codes[rows, :].bitcast(FP8X4), rhs_scale=q_scales[rows, :],
                                     start=True, stop=True)
-
-        def sigmoid(n):
-            g, b, a = place(n)
-            nc.scalar.activation(out=p_sb[n][:].rearrange("p (c r i) -> p c r i", r=PACK, i=2),
-                                 in_=score[a][b % 2][:].rearrange("p r (c i) -> p c r i", i=2), func=ACT.Sigmoid)
+            nc.scalar.activation(out=p_sb[n][:].rearrange("s (c r e) -> s c r e", r=PACK, e=2),
+                                 in_=bank[:].rearrange("s r (c e) -> s c r e", e=2), func=ACT.Sigmoid)
 
         def weigh(n):
             g, b, a = place(n)
+            pairs = slice(QB // 2 * (b % 2), QB // 2 * (b % 2 + 1))
             nc.vector.tensor_tensor(
-                out=w_mx[n][0][:].rearrange("p (c i r) -> p c r i", i=2, r=PACK),
-                in0=p_sb[n][:].rearrange("p (c r i) -> p c r i", r=PACK, i=2),
-                in1=mt[b // 2][:, :, QB * (b % 2):QB * (b % 2 + 1)].rearrange("p r (c i) -> p c r i", i=2),
+                out=w_mx[n // 4][a][0][:].rearrange("s (e c r) -> s c r e", e=2, r=PACK)[:, pairs],
+                in0=p_sb[n][:].rearrange("s (c r e) -> s c r e", r=PACK, e=2),
+                in1=mt[b // 2][:, :, QB * (b % 2):QB * (b % 2 + 1)].rearrange("s r (c e) -> s c r e", e=2),
                 op=ALU.mult)
 
-        def values(n):
-            g, b, a = place(n)
-            cols = slice(E * a, E * (a + 1))
-            nc.tensor.matmul_mx(out=y_ps[n // 4][:, n % 4, :],
-                                lhsT=w_mx[n][1][:].bitcast(FP8X4), lhsT_scale=w_mx[n][2][:],
-                                rhs=v_mx[g][1][:, cols].bitcast(FP8X4), rhs_scale=v_mx[g][2][:, cols],
-                                start=True, stop=True)
+        def times_v(f, a):
+            w_codes, w_scales = w_mx[f][a][1], w_mx[f][a][2]
+            v_codes, v_scales = v_mx[f // 2][1], v_mx[f // 2][2]
+            v_cols = slice(E * a, E * (a + 1))
+            for e in range(2):
+                cols = slice(QB * e, QB * (e + 1))
+                nc.tensor.matmul_mx(out=y_ps[f][:, 2 * a + e, :],
+                                    lhsT=w_codes[:, cols].bitcast(FP8X4), lhsT_scale=w_scales[:, cols],
+                                    rhs=v_codes[:, v_cols].bitcast(FP8X4), rhs_scale=v_scales[:, v_cols],
+                                    start=True, stop=True)
 
-        def squares(f):
-            for n in range(4 * f, 4 * f + 4):
-                nc.scalar.activation(out=sq_sb[n][:], in_=y_ps[f][:, n % 4, :], func=ACT.Square,
-                                     accum_out=ssq[f][:, n % 4:n % 4 + 1])
+        def add_squares(f, a):
+            for m in range(2 * a, 2 * a + 2):
+                nc.scalar.activation(out=y_squared[4 * f + m][:], in_=y_ps[f][:, m, :], func=ACT.Square,
+                                     accum_out=sum_squares[f][:, m:m + 1])
 
         def inverse_root(f):
-            nc.scalar.activation(out=rstd[f][:], in_=ssq[f][:], func=ACT.Abs_reciprocal_sqrt,
-                                 scale=1.0 / E, bias=256.0 * EPS)
+            nc.scalar.activation(out=inv_root[f][:], in_=sum_squares[f][:], func=ACT.Abs_reciprocal_sqrt,
+                                 scale=1.0 / E, bias=Y_DIVISOR * Y_DIVISOR * EPS)
 
-        def finish(f):
+        def normalise_and_store(f):
             for a in range(2):
-                for b in range(2):
-                    m = 2 * b + a
-                    nc.vector.scalar_tensor_tensor(out=o_sb[f][a][:, b, :], in0=y_ps[f][:, m, :],
-                                                   scalar=rstd[f][:, m:m + 1], in1=gn_sb[:],
+                for e in range(2):
+                    m = 2 * a + e
+                    nc.vector.scalar_tensor_tensor(out=o_sb[f][a][:, E * e:E * (e + 1)], in0=y_ps[f][:, m, :],
+                                                   scalar=inv_root[f][:, m:m + 1], in1=gn_sb[:],
                                                    op0=ALU.mult, op1=ALU.mult)
                 rows = out[2 * (f // 2) + a, HALF * (f % 2):HALF * (f % 2 + 1), :]
-                nc.sync.dma_start(out=rows.rearrange("(b p) e -> p b e", b=2), in_=o_sb[f][a][:])
+                nc.sync.dma_start(out=rows.rearrange("(c e) x -> c (e x)", e=2), in_=o_sb[f][a][:])
 
-        nc.scalar.dma_start(out=t_sb[:], in_=t.rearrange("(p r) o -> p (r o)", r=PACK))
-        load_pair(kT, 0, slice(0, N), k_raw[0])
-        load_q(0, 0)
+        nc.vector.memset(warm_in[:], 0.0)
+        nc.scalar.dma_start(out=t_sb[:], in_=t.rearrange("(s r) o -> s (r o)", r=PACK))
+        nc.scalar.activation(out=warm_out[:], in_=warm_in[:], func=ACT.Sigmoid)
+
+        load_features(kT, 0, k_raw[0])
+        load_features(qT, 0, q_raw[0])
         load_mask(0)
-        load_q(0, 1)
         load_mask(1)
-        load_pair(kT, 1, slice(0, N), k_raw[1])
-        load_q(1, 0)
-        load_q(1, 1)
+        load_features(kT, 1, k_raw[1])
+        load_features(qT, 1, q_raw[1])
         load_v(0)
         load_v(1)
         nc.sync.dma_start(out=gn_sb[:], in_=gn[:, :])
 
-        pack_k(0, 0, False)
-        pack_k(0, 1, True)
+        pack_k(0, 0, on_vector)
+        pack_k(0, 1, on_scalar)
         quantize(k_mx[0][0])
         quantize(k_mx[0][1])
-        pack_q(0, 0, False)
-        pack_q(0, 1, True)
+        pack_q(0, 0, on_vector)
+        pack_q(0, 1, on_scalar)
+        pack_q(0, 3, on_scalar)
         quantize(q_mx[0][0])
-        scores(0)
-        scores(1)
         quantize(q_mx[0][1])
-        scores(2)
-        scores(3)
-        mask_times_t(0)
+        pack_q(0, 2, on_vector)
+        mask_times_t(0, 0)
+        quantize(q_mx[0][2])
+        mask_times_t(0, 1)
+        mask_times_t(1, 0)
+        quantize(q_mx[0][3])
 
-        scalar_side = {
-            2: [lambda: pack_q(0, 2, True)],
-            3: [lambda: pack_q(0, 3, True)],
-            6: [lambda: pack_k(1, 1, True)],
-            7: [lambda: pack_q(1, 1, True)],
-            9: [lambda: pack_q(1, 2, True)],
-            10: [lambda: pack_q(1, 3, True)],
-        }
-        vector_side = {
-            2: [lambda: quantize(q_mx[0][2])],
-            3: [lambda: quantize(q_mx[0][3]), lambda: mask_times_t(1)],
-            5: [lambda: pack_k(1, 0, False)],
-            6: [lambda: quantize(k_mx[1][0]), lambda: pack_q(1, 0, False), lambda: quantize(k_mx[1][1]),
-                lambda: quantize(q_mx[1][0])],
-            7: [lambda: quantize(q_mx[1][1])],
-            9: [lambda: quantize(q_mx[1][2])],
-            10: [lambda: quantize(q_mx[1][3]), lambda: pack_v(0, 0, False), lambda: pack_v(0, 1, False)],
-            11: [lambda: quantize(v_mx[0]), lambda: pack_v(1, 0, False), lambda: pack_v(1, 1, False)],
-            12: [lambda: quantize(v_mx[1])],
-        }
-        for n in range(16):
-            for job in scalar_side.get(n, []):
-                job()
-            sigmoid(n)
-            for job in vector_side.get(n, []):
-                job()
-            if 4 <= n + 2 < 16:
-                scores(n + 2)
+        for n in range(0, 5):
+            sigmoid_scores(n)
+        pack_k(1, 1, on_scalar)
+        for n in range(5, 8):
+            sigmoid_scores(n)
+        pack_q(1, 1, on_scalar)
+        pack_q(1, 2, on_scalar)
+
+        weigh(0)
+        mask_times_t(1, 1)
+        weigh(1)
+        weigh(2)
+        pack_k(1, 0, on_vector)
+        weigh(3)
+        quantize(k_mx[1][0])
+        quantize(w_mx[0][0])
+        quantize(k_mx[1][1])
+        pack_q(1, 0, on_vector)
+        quantize(w_mx[0][1])
+        for b in range(3):
+            quantize(q_mx[1][b])
+            weigh(4 + b)
+        weigh(7)
+        quantize(w_mx[1][0])
+
+        sigmoid_scores(8)
+        sigmoid_scores(9)
+        pack_q(1, 3, on_scalar)
+        pack_v(0, 0, on_scalar)
+        for n in range(10, 14):
+            sigmoid_scores(n)
+        weigh(8)
+        quantize(q_mx[1][3])
+        sigmoid_scores(14)
+        sigmoid_scores(15)
+
+        quantize(w_mx[1][1])
+        pack_v(0, 1, on_vector)
+        weigh(9)
+        quantize(v_mx[0])
+        pack_v(1, 0, on_vector)
+        pack_v(1, 1, on_vector)
+        weigh(10)
+        quantize(v_mx[1])
+        weigh(11)
+        quantize(w_mx[2][0])
+        weigh(12)
+        quantize(w_mx[2][1])
+        for n in range(13, 16):
             weigh(n)
-            if n >= 1:
-                quantize(w_mx[n - 1])
-            if n == 13:
-                for m in range(12):
-                    values(m)
-                squares(0)
-            if n == 14:
-                squares(1)
-        quantize(w_mx[15])
-        for m in range(12, 16):
-            values(m)
+        quantize(w_mx[3][0])
+        quantize(w_mx[3][1])
+
+        for f in range(2):
+            times_v(f, 0)
+            times_v(f, 1)
+            add_squares(f, 0)
+            add_squares(f, 1)
+        times_v(2, 0)
+        add_squares(2, 0)
         inverse_root(0)
         inverse_root(1)
-        finish(0)
-        squares(2)
+        times_v(2, 1)
+        add_squares(2, 1)
         inverse_root(2)
-        finish(1)
-        squares(3)
+        times_v(3, 0)
+        times_v(3, 1)
+        add_squares(3, 0)
+        add_squares(3, 1)
         inverse_root(3)
-        finish(2)
-        finish(3)
+        for f in range(PHASES):
+            normalise_and_store(f)

from contextlib import ExitStack

import concourse.mybir as mybir

H, D, NQ, N, E = 4, 256, 512, 512, 128
FLOPS = 2 * H * N * NQ * (D + E)

F32 = mybir.dt.float32
BF16 = mybir.dt.bfloat16
U32 = mybir.dt.uint32
U8 = mybir.dt.uint8
FP8X4 = mybir.dt.float8_e4m3fn_x4
ACT = mybir.ActivationFunctionType
ALU = mybir.AluOpType

P = 128
PACK = 4
ROWS = D // PACK
QB = 128
HALF = 2 * QB
PAIRS = H // 2
PHASES = 4
UNITS = 16
Y_DIVISOR = 16.0
EPS = 1e-5


def tile_rows_a_sigmoid_mask_onorm_kernel(tc, qT, kT, t, v, mask, gn, out):
    nc = tc.nc
    with ExitStack() as ctx:
        sb = ctx.enter_context(tc.tile_pool(name="sb", bufs=1))
        ps = ctx.enter_context(tc.psum_pool(name="ps", bufs=1))
        ctx.enter_context(tc.manual_schedule())

        def sbuf(name, shape, dtype):
            return sb.tile(shape, dtype, name=name, align_bytes=64)

        def mx_tiles(name, cols):
            return (sbuf(name + "_bf", [P, PACK * cols], BF16), sbuf(name + "_codes", [P, cols], U32),
                    sbuf(name + "_scales", [P, cols], U8))

        k_raw = [sbuf("k_raw%d" % g, [P, PACK, N], F32) for g in range(PAIRS)]
        q_raw = [sbuf("q_raw%d" % g, [P, PACK, NQ], F32) for g in range(PAIRS)]
        v_raw = [sbuf("v_raw%d" % g, [P, 2, PACK * E], F32) for g in range(PAIRS)]
        m_raw = [sbuf("m_raw%d" % rh, [P, 2, NQ], F32) for rh in range(2)]
        mt = [sbuf("mt%d" % u, [P, PACK, HALF], F32) for u in range(2)]
        t_sb = sbuf("t_sb", [P, PACK], F32)
        gn_sb = sbuf("gn_sb", [P, E], F32)
        k_mx = [[mx_tiles("k%d%d" % (g, rh), 2 * P) for rh in range(2)] for g in range(PAIRS)]
        q_mx = [[mx_tiles("q%d%d" % (g, b), QB) for b in range(NQ // QB)] for g in range(PAIRS)]
        v_mx = [mx_tiles("v%d" % g, 2 * E) for g in range(PAIRS)]
        w_mx = [[mx_tiles("w%d%d" % (f, a), HALF) for a in range(2)] for f in range(PHASES)]
        p_sb = [sbuf("p%d" % n, [P, PACK * QB], F32) for n in range(UNITS)]
        y_squared = [sbuf("y_squared%d" % n, [P, E], F32) for n in range(UNITS)]
        sum_squares = [sbuf("sum_squares%d" % f, [P, 4], F32) for f in range(PHASES)]
        inv_root = [sbuf("inv_root%d" % f, [P, 4], F32) for f in range(PHASES)]
        o_sb = [[sbuf("o%d%d" % (f, a), [P, 2 * E], F32) for a in range(2)] for f in range(PHASES)]
        warm_in = sbuf("warm_in", [P, 8], F32)
        warm_out = sbuf("warm_out", [P, 8], F32)
        score = [[ps.tile([P, PACK, QB], F32, name="score%d%d" % (a, x)) for x in range(2)] for a in range(2)]
        y_ps = [ps.tile([P, 4, E], F32, name="y%d" % f) for f in range(PHASES)]

        def load_features(src, g, dst):
            rows = src[2 * g:2 * g + 2].rearrange("h (p j) c -> (h p) j c", j=PACK)
            nc.sync.dma_start(out=dst[:], in_=rows)

        def load_mask(rh):
            rows = mask.rearrange("(s r) q -> s r q", r=PACK)[:, 2 * rh:2 * rh + 2, :]
            nc.sync.dma_start(out=m_raw[rh][:], in_=rows)

        def load_v(g):
            nc.sync.dma_start(out=v_raw[g][:], in_=v[2 * g:2 * g + 2].rearrange("h (s r) e -> s h (r e)", r=PACK))

        def on_vector(dst, src):
            nc.vector.tensor_copy(out=dst, in_=src)

        def on_scalar(dst, src):
            nc.scalar.copy(out=dst, in_=src)

        def pack_k(g, rh, copy):
            src = k_raw[g][:].rearrange("p j (s rh x) -> p rh s j x", rh=2, x=2)[:, rh]
            copy(k_mx[g][rh][0][:].rearrange("p (x s j) -> p s j x", x=2, j=PACK), src)

        def pack_q(g, b, copy):
            src = q_raw[g][:, :, QB * b:QB * (b + 1)].rearrange("p j (c x) -> p c j x", x=2)
            copy(q_mx[g][b][0][:].rearrange("p (c x j) -> p c j x", x=2, j=PACK), src)

        def pack_v(g, a, copy):
            src = v_raw[g][:, a, :].rearrange("s (r c x) -> s c r x", r=PACK, x=2)
            dst = v_mx[g][0][:, PACK * E * a:PACK * E * (a + 1)]
            copy(dst.rearrange("s (c x r) -> s c r x", x=2, r=PACK), src)

        def quantize(operand):
            values_bf, codes, scales = operand
            nc.vector.quantize_mx(out=codes[:].bitcast(FP8X4), scales=scales[:], in_=values_bf[:])

        def mask_times_t(rh, u):
            for x in range(2):
                r = 2 * rh + x
                nc.vector.tensor_scalar(out=mt[u][:, r, :], in0=m_raw[rh][:, x, HALF * u:HALF * (u + 1)],
                                        scalar1=t_sb[:, r:r + 1], scalar2=None, op0=ALU.mult)

        def place(n):
            return n // 8, (n // 2) % 4, n % 2

        def sigmoid_scores(n):
            g, b, a = place(n)
            bank = score[a][b % 2]
            rows = slice(ROWS * a, ROWS * (a + 1))
            q_codes, q_scales = q_mx[g][b][1], q_mx[g][b][2]
            for r in range(PACK):
                k_codes, k_scales = k_mx[g][r // 2][1], k_mx[g][r // 2][2]
                cols = slice(P * (r % 2), P * (r % 2 + 1))
                nc.tensor.matmul_mx(out=bank[:, r, :],
                                    lhsT=k_codes[rows, cols].bitcast(FP8X4), lhsT_scale=k_scales[rows, cols],
                                    rhs=q_codes[rows, :].bitcast(FP8X4), rhs_scale=q_scales[rows, :],
                                    start=True, stop=True)
            nc.scalar.activation(out=p_sb[n][:].rearrange("s (c r e) -> s c r e", r=PACK, e=2),
                                 in_=bank[:].rearrange("s r (c e) -> s c r e", e=2), func=ACT.Sigmoid)

        def weigh(n):
            g, b, a = place(n)
            pairs = slice(QB // 2 * (b % 2), QB // 2 * (b % 2 + 1))
            nc.vector.tensor_tensor(
                out=w_mx[n // 4][a][0][:].rearrange("s (e c r) -> s c r e", e=2, r=PACK)[:, pairs],
                in0=p_sb[n][:].rearrange("s (c r e) -> s c r e", r=PACK, e=2),
                in1=mt[b // 2][:, :, QB * (b % 2):QB * (b % 2 + 1)].rearrange("s r (c e) -> s c r e", e=2),
                op=ALU.mult)

        def times_v(f, a):
            w_codes, w_scales = w_mx[f][a][1], w_mx[f][a][2]
            v_codes, v_scales = v_mx[f // 2][1], v_mx[f // 2][2]
            v_cols = slice(E * a, E * (a + 1))
            for e in range(2):
                cols = slice(QB * e, QB * (e + 1))
                nc.tensor.matmul_mx(out=y_ps[f][:, 2 * a + e, :],
                                    lhsT=w_codes[:, cols].bitcast(FP8X4), lhsT_scale=w_scales[:, cols],
                                    rhs=v_codes[:, v_cols].bitcast(FP8X4), rhs_scale=v_scales[:, v_cols],
                                    start=True, stop=True)

        def add_squares(f, a):
            for m in range(2 * a, 2 * a + 2):
                nc.scalar.activation(out=y_squared[4 * f + m][:], in_=y_ps[f][:, m, :], func=ACT.Square,
                                     accum_out=sum_squares[f][:, m:m + 1])

        def inverse_root(f):
            nc.scalar.activation(out=inv_root[f][:], in_=sum_squares[f][:], func=ACT.Abs_reciprocal_sqrt,
                                 scale=1.0 / E, bias=Y_DIVISOR * Y_DIVISOR * EPS)

        def normalise_and_store(f):
            for a in range(2):
                for e in range(2):
                    m = 2 * a + e
                    nc.vector.scalar_tensor_tensor(out=o_sb[f][a][:, E * e:E * (e + 1)], in0=y_ps[f][:, m, :],
                                                   scalar=inv_root[f][:, m:m + 1], in1=gn_sb[:],
                                                   op0=ALU.mult, op1=ALU.mult)
                rows = out[2 * (f // 2) + a, HALF * (f % 2):HALF * (f % 2 + 1), :]
                nc.sync.dma_start(out=rows.rearrange("(c e) x -> c (e x)", e=2), in_=o_sb[f][a][:])

        nc.vector.memset(warm_in[:], 0.0)
        nc.scalar.dma_start(out=t_sb[:], in_=t.rearrange("(s r) o -> s (r o)", r=PACK))
        nc.scalar.activation(out=warm_out[:], in_=warm_in[:], func=ACT.Sigmoid)

        load_features(kT, 0, k_raw[0])
        load_features(qT, 0, q_raw[0])
        load_mask(0)
        load_mask(1)
        load_features(kT, 1, k_raw[1])
        load_features(qT, 1, q_raw[1])
        load_v(0)
        load_v(1)
        nc.sync.dma_start(out=gn_sb[:], in_=gn[:, :])

        pack_k(0, 0, on_vector)
        pack_k(0, 1, on_scalar)
        quantize(k_mx[0][0])
        quantize(k_mx[0][1])
        pack_q(0, 0, on_vector)
        pack_q(0, 1, on_scalar)
        pack_q(0, 3, on_scalar)
        quantize(q_mx[0][0])
        quantize(q_mx[0][1])
        pack_q(0, 2, on_vector)
        mask_times_t(0, 0)
        quantize(q_mx[0][2])
        mask_times_t(0, 1)
        mask_times_t(1, 0)
        quantize(q_mx[0][3])

        for n in range(0, 5):
            sigmoid_scores(n)
        pack_k(1, 1, on_scalar)
        for n in range(5, 8):
            sigmoid_scores(n)
        pack_q(1, 1, on_scalar)
        pack_q(1, 2, on_scalar)

        weigh(0)
        mask_times_t(1, 1)
        weigh(1)
        weigh(2)
        pack_k(1, 0, on_vector)
        weigh(3)
        quantize(k_mx[1][0])
        quantize(w_mx[0][0])
        quantize(k_mx[1][1])
        pack_q(1, 0, on_vector)
        quantize(w_mx[0][1])
        for b in range(3):
            quantize(q_mx[1][b])
            weigh(4 + b)
        weigh(7)
        quantize(w_mx[1][0])

        sigmoid_scores(8)
        sigmoid_scores(9)
        pack_q(1, 3, on_scalar)
        pack_v(0, 0, on_scalar)
        for n in range(10, 14):
            sigmoid_scores(n)
        weigh(8)
        quantize(q_mx[1][3])
        sigmoid_scores(14)
        sigmoid_scores(15)

        quantize(w_mx[1][1])
        pack_v(0, 1, on_vector)
        weigh(9)
        quantize(v_mx[0])
        pack_v(1, 0, on_vector)
        pack_v(1, 1, on_vector)
        weigh(10)
        quantize(v_mx[1])
        weigh(11)
        quantize(w_mx[2][0])
        weigh(12)
        quantize(w_mx[2][1])
        for n in range(13, 16):
            weigh(n)
        quantize(w_mx[3][0])
        quantize(w_mx[3][1])

        for f in range(2):
            times_v(f, 0)
            times_v(f, 1)
            add_squares(f, 0)
            add_squares(f, 1)
        times_v(2, 0)
        add_squares(2, 0)
        inverse_root(0)
        inverse_root(1)
        times_v(2, 1)
        add_squares(2, 1)
        inverse_root(2)
        times_v(3, 0)
        times_v(3, 1)
        add_squares(3, 0)
        add_squares(3, 1)
        inverse_root(3)
        for f in range(PHASES):
            normalise_and_store(f)
